import numpy as np
import ml_dtypes


def mxq(x, axis, fmt="e4m3"):
    dtype, down = {"e4m3": (ml_dtypes.float8_e4m3fn, 7), "e5m2": (ml_dtypes.float8_e5m2, 14)}[fmt]
    v = np.moveaxis(np.asarray(x, np.float32).astype(ml_dtypes.bfloat16).astype(np.float64), axis, -1)
    blocks = v.reshape(v.shape[:-1] + (-1, 32))
    amax = np.abs(blocks).max(-1, keepdims=True)
    byte = np.maximum(np.where(amax > 0, np.frexp(amax)[1] - 1 + 127, 0) - down, 1)
    scale = np.exp2(byte - 127.0)
    codes = (blocks / scale).astype(np.float32).astype(dtype).astype(np.float64)
    return np.moveaxis((codes * scale).reshape(v.shape), -1, axis)


WIDE = False


def mx_kscale(k):
    if not WIDE:
        return np.ones(k)
    levels = np.array([10, -10, 5, -5, 0])
    if k % 512:
        return np.exp2(np.random.permutation(np.resize(levels, k // 32))).repeat(32)
    a = np.empty((k // 512, 16))
    for p in range(k // 512):
        a[p, :8] = np.random.permutation(np.resize(levels, 8))
        for g in range(8):
            far = levels[np.abs(levels - a[p, g]) >= 10]
            a[p, g + 8] = far[np.random.randint(len(far))]
    return np.exp2(a.ravel()).repeat(32)


def f64(x):
    return np.asarray(x).astype(np.float64)


def striped(idx):
    return np.tile(idx.reshape(-1, 16).T, (8, 1)).astype(np.uint16)


def unstriped(offs):
    return offs[:16].T.reshape(-1).astype(np.int64)


def gelu(v):
    return 0.5 * v * (1.0 + np.tanh(np.sqrt(2.0 / np.pi) * (v + 0.044715 * v**3)))


K, T, S, H, N = 1024, 1024, 512, 512, 128


def setup_inputs():
    n = np.random.standard_normal
    s = mx_kscale(K)[:, None]
    u = mx_kscale(H)
    return {
        "xT": (n((K, T)) * s).astype(np.float32),
        "w1": (n((K, N)) / np.sqrt(2 * K) / s).astype(np.float32),
        "w2": (n((K, H)) / np.sqrt(K) / s * u).astype(np.float32),
        "w3": (n((H, N)) / np.sqrt(2 * H) / u[:, None]).astype(np.float32),
        "offs": striped(np.random.permutation(T)[:S]),
    }


def reference(xT, w1, w2, w3, offs):
    xq = mxq(f64(xT)[:, unstriped(offs)], 0, "e4m3")
    h = gelu(mxq(f64(w2), 0, "e4m3").T @ xq)
    return mxq(f64(w1), 0, "e4m3").T @ xq + mxq(f64(w3), 0, "e4m3").T @ mxq(h, 0, "e4m3")

@@ -1,0 +1,127 @@
+from contextlib import ExitStack
+
+import concourse.mybir as mybir
+
+K, T, S, H, N = 1024, 1024, 512, 512, 128
+FLOPS = 2 * S * (K * H + K * N + H * N)
+
+F32 = mybir.dt.float32
+BF16 = mybir.dt.bfloat16
+U32 = mybir.dt.uint32
+U16 = mybir.dt.uint16
+U8 = mybir.dt.uint8
+FP8X4 = mybir.dt.float8_e4m3fn_x4
+GELU = mybir.ActivationFunctionType.Gelu_apprx_tanh
+
+P = 128
+PACK = 4
+K_PASS = P * PACK
+PASSES = K // K_PASS
+CHUNK = 128
+CHUNKS = S // CHUNK
+X_VECTOR_TOKENS = 256
+W2_VECTOR_COLS = (48, 84)
+
+
+def tile_picked_lora_gelu_e_kernel(tc, xT, w1, w2, w3, offs, out):
+    nc = tc.nc
+
+    with ExitStack() as ctx:
+        sb = ctx.enter_context(tc.tile_pool(name="sb", bufs=1))
+        psum = ctx.enter_context(tc.psum_pool(name="psum", bufs=1))
+
+        def sbuf(name, shape, dtype):
+            return sb.tile(shape, dtype, name=name, align_bytes=64)
+
+        def quantise(name, grouped, words):
+            codes = sbuf(name + "_codes", [P, words], U32)
+            scales = sbuf(name + "_scales", [P, words], U8)
+            nc.vector.quantize_mx(out=codes[:].bitcast(FP8X4), scales=scales[:], in_=grouped)
+            return codes, scales
+
+        def mx_pass(dst, stationary, s_cols, moving, m_cols, start, stop):
+            nc.tensor.matmul_mx(
+                out=dst,
+                lhsT=stationary[0][:, s_cols].bitcast(FP8X4),
+                lhsT_scale=stationary[1][:, s_cols],
+                rhs=moving[0][:, m_cols].bitcast(FP8X4),
+                rhs_scale=moving[1][:, m_cols],
+                start=start,
+                stop=stop,
+            )
+
+        offsets = sb.tile([P, S // 16], U16, name="offsets")
+        x_rows = xT.rearrange("(z p u e) t -> z u p e t", z=PASSES, p=P, u=2)
+        x_raw = {}
+        for z in range(PASSES):
+            for u in range(2):
+                x_raw[z, u] = sbuf("x_raw%d%d" % (z, u), [P, 2, T], F32)
+                nc.sync.dma_start(out=x_raw[z, u][:], in_=x_rows[z, u])
+                if (z, u) == (0, 0):
+                    nc.sync.dma_start(offsets[:], offs)
+        w2_raw = []
+        for z in range(PASSES):
+            w2_raw.append(sbuf("w2_raw%d" % z, [P, PACK, H], F32))
+            nc.sync.dma_start(out=w2_raw[z][:], in_=w2[z * K_PASS : (z + 1) * K_PASS, :].rearrange("(p j) c -> p j c", j=PACK))
+        w1_raw = sbuf("w1_raw", [P, PASSES, PACK, N], F32)
+        nc.sync.dma_start(out=w1_raw[:], in_=w1.rearrange("(z p j) n -> p z j n", z=PASSES, j=PACK))
+        w3_raw = sbuf("w3_raw", [P, PACK, N], F32)
+        nc.sync.dma_start(out=w3_raw[:], in_=w3.rearrange("(p j) n -> p j n", j=PACK))
+
+        warm_in = sbuf("warm_in", [P, 16], F32)
+        warm_out = sbuf("warm_out", [P, 16], F32)
+        nc.vector.memset(warm_in[:], 0.0)
+        nc.scalar.activation(warm_out[:], warm_in[:], GELU)
+
+        xq = []
+        for z in range(PASSES):
+            picked = sbuf("picked%d" % z, [P, S, 2], U32)
+            for u in range(2):
+                pairs = sbuf("pairs%d%d" % (z, u), [P, T * 2], BF16)
+                dst = pairs[:].rearrange("p (t e) -> p t e", e=2)
+                src = x_raw[z, u][:].rearrange("p e t -> p t e")
+                nc.scalar.copy(out=dst[:, X_VECTOR_TOKENS:, :], in_=src[:, X_VECTOR_TOKENS:, :])
+                nc.vector.tensor_copy(out=dst[:, :X_VECTOR_TOKENS, :], in_=src[:, :X_VECTOR_TOKENS, :])
+                nc.vector.tensor_copy(out=picked[:, :, u], in_=pairs[:].bitcast(U32).indirect(offsets[:]))
+            xq.append(quantise("x%d" % z, picked[:].rearrange("p s u -> p (s u)").bitcast(BF16), S))
+
+        hidden = [psum.tile([P, PACK, CHUNK], F32, name="hidden%d" % c) for c in range(CHUNKS)]
+        for z in range(PASSES):
+            grouped = sbuf("w2_grouped%d" % z, [P, PACK, P * PACK], BF16)
+            dst = grouped[:].rearrange("p t (m j) -> p m j t", j=PACK)
+            src = w2_raw[z][:].rearrange("p j (m t) -> p m j t", t=PACK)
+            split = W2_VECTOR_COLS[z]
+            nc.scalar.copy(out=dst[:, split:], in_=src[:, split:])
+            nc.vector.tensor_copy(out=dst[:, :split], in_=src[:, :split])
+            w2q = [quantise("w2_%d%d" % (z, t), grouped[:, t, :], P) for t in range(PACK)]
+            for c in range(CHUNKS):
+                for t in range(PACK):
+                    mx_pass(hidden[c][:, t, :], w2q[t], slice(0, P), xq[z], slice(c * CHUNK, (c + 1) * CHUNK),
+                            start=(z == 0 and t == 0), stop=(z == PASSES - 1 and t == PACK - 1))
+
+        w1_grouped = sbuf("w1_grouped", [P, PASSES * N * PACK], BF16)
+        nc.vector.tensor_copy(
+            out=w1_grouped[:].rearrange("p (z c i j) -> p z c j i", z=PASSES, i=4, j=PACK),
+            in_=w1_raw[:].rearrange("p z j (c i) -> p z c j i", i=4),
+        )
+        w3_grouped = sbuf("w3_grouped", [P, N * PACK], BF16)
+        nc.vector.tensor_copy(
+            out=w3_grouped[:].rearrange("p (c i j) -> p c j i", i=4, j=PACK),
+            in_=w3_raw[:].rearrange("p j (c i) -> p c j i", i=4),
+        )
+        w1q = quantise("w1", w1_grouped[:], PASSES * N)
+        w3q = quantise("w3", w3_grouped[:], N)
+
+        acc = [psum.tile([P, CHUNK], F32, name="acc%d" % c) for c in range(CHUNKS)]
+        for c in range(CHUNKS):
+            for z in range(PASSES):
+                mx_pass(acc[c][:], w1q, slice(z * N, (z + 1) * N), xq[z], slice(c * CHUNK, (c + 1) * CHUNK), start=(z == 0), stop=False)
+
+        for c in range(CHUNKS):
+            act = sbuf("act%d" % c, [P, CHUNK * PACK], BF16)
+            nc.scalar.activation(act[:].rearrange("p (n t) -> p n t", t=PACK), hidden[c][:].rearrange("p t n -> p n t"), GELU)
+            hq = quantise("h%d" % c, act[:], CHUNK)
+            mx_pass(acc[c][:], w3q, slice(0, N), hq, slice(0, CHUNK), start=False, stop=True)
+            result = sbuf("result%d" % c, [P, CHUNK], F32)
+            nc.vector.tensor_copy(out=result[:], in_=acc[c][:])
+            nc.sync.dma_start(out=out[:, c * CHUNK : (c + 1) * CHUNK], in_=result[:])

@@ -8,6 +8,7 @@ FLOPS = 2 * S * (K * H + K * N + H * N)
 F32 = mybir.dt.float32
 BF16 = mybir.dt.bfloat16
 U32 = mybir.dt.uint32
+I32 = mybir.dt.int32
 U16 = mybir.dt.uint16
 U8 = mybir.dt.uint8
 FP8X4 = mybir.dt.float8_e4m3fn_x4
@@ -19,8 +20,9 @@ K_PASS = P * PACK
 PASSES = K // K_PASS
 CHUNK = 128
 CHUNKS = S // CHUNK
-X_VECTOR_TOKENS = 256
-W2_VECTOR_COLS = (48, 84)
+X_VECTOR_TOKENS = (640, 640, 544, 448)
+W2_VECTOR_COLS = (32, 32)
+HALF = S // 2
 
 
 def tile_picked_lora_gelu_e_kernel(tc, xT, w1, w2, w3, offs, out):
@@ -32,6 +34,11 @@ def tile_picked_lora_gelu_e_kernel(tc, xT, w1, w2, w3, offs, out):
 
         def sbuf(name, shape, dtype):
             return sb.tile(shape, dtype, name=name, align_bytes=64)
+
+        def load(slot, shape, rows):
+            raw = sbuf(slot, shape, F32)
+            nc.sync.dma_start(out=raw[:], in_=rows)
+            return raw
 
         def quantise(name, grouped, words):
             codes = sbuf(name + "_codes", [P, words], U32)
@@ -50,61 +57,85 @@ def tile_picked_lora_gelu_e_kernel(tc, xT, w1, w2, w3, offs, out):
                 stop=stop,
             )
 
-        offsets = sb.tile([P, S // 16], U16, name="offsets")
+        def shared_cast(dst, src, split):
+            nc.scalar.copy(out=dst[:, split:], in_=src[:, split:])
+            if split:
+                nc.vector.tensor_copy(out=dst[:, :split], in_=src[:, :split])
+
         x_rows = xT.rearrange("(z p u e) t -> z u p e t", z=PASSES, p=P, u=2)
-        x_raw = {}
-        for z in range(PASSES):
-            for u in range(2):
-                x_raw[z, u] = sbuf("x_raw%d%d" % (z, u), [P, 2, T], F32)
-                nc.sync.dma_start(out=x_raw[z, u][:], in_=x_rows[z, u])
-                if (z, u) == (0, 0):
-                    nc.sync.dma_start(offsets[:], offs)
-        w2_raw = []
-        for z in range(PASSES):
-            w2_raw.append(sbuf("w2_raw%d" % z, [P, PACK, H], F32))
-            nc.sync.dma_start(out=w2_raw[z][:], in_=w2[z * K_PASS : (z + 1) * K_PASS, :].rearrange("(p j) c -> p j c", j=PACK))
-        w1_raw = sbuf("w1_raw", [P, PASSES, PACK, N], F32)
-        nc.sync.dma_start(out=w1_raw[:], in_=w1.rearrange("(z p j) n -> p z j n", z=PASSES, j=PACK))
-        w3_raw = sbuf("w3_raw", [P, PACK, N], F32)
-        nc.sync.dma_start(out=w3_raw[:], in_=w3.rearrange("(p j) n -> p j n", j=PACK))
+
+        def token_pairs(z, u, raw_slot, window_slot):
+            raw = load(raw_slot, [P, 2, T], x_rows[z, u])
+            window = sbuf(window_slot, [P, 2 * T], BF16)
+            shared_cast(window[:].rearrange("p (t e) -> p t e", e=2), raw[:].rearrange("p e t -> p t e"), X_VECTOR_TOKENS[2 * z + u])
+            return window[:].bitcast(U32)
+
+        def cast_w2(z, raw_slot, grouped_slot):
+            raw = load(raw_slot, [P, PACK, H], w2[z * K_PASS : (z + 1) * K_PASS, :].rearrange("(p j) c -> p j c", j=PACK))
+            grouped = sbuf(grouped_slot, [P, H * PACK], BF16)
+            shared_cast(
+                grouped[:].rearrange("p (t m j) -> p m j t", t=PACK, j=PACK),
+                raw[:].rearrange("p j (m t) -> p m j t", t=PACK),
+                W2_VECTOR_COLS[z],
+            )
+            return grouped
+
+        def quantise_w2(z, grouped):
+            return [quantise("w2_%d%d" % (z, t), grouped[:, t * K_PASS : (t + 1) * K_PASS], P) for t in range(PACK)]
+
+        offsets = sb.tile([P, S // 16], U16, name="offsets")
+        nc.sync.dma_start(offsets[:], offs)
 
         warm_in = sbuf("warm_in", [P, 16], F32)
         warm_out = sbuf("warm_out", [P, 16], F32)
         nc.vector.memset(warm_in[:], 0.0)
         nc.scalar.activation(warm_out[:], warm_in[:], GELU)
 
-        xq = []
-        for z in range(PASSES):
-            picked = sbuf("picked%d" % z, [P, S, 2], U32)
-            for u in range(2):
-                pairs = sbuf("pairs%d%d" % (z, u), [P, T * 2], BF16)
-                dst = pairs[:].rearrange("p (t e) -> p t e", e=2)
-                src = x_raw[z, u][:].rearrange("p e t -> p t e")
-                nc.scalar.copy(out=dst[:, X_VECTOR_TOKENS:, :], in_=src[:, X_VECTOR_TOKENS:, :])
-                nc.vector.tensor_copy(out=dst[:, :X_VECTOR_TOKENS, :], in_=src[:, :X_VECTOR_TOKENS, :])
-                nc.vector.tensor_copy(out=picked[:, :, u], in_=pairs[:].bitcast(U32).indirect(offsets[:]))
-            xq.append(quantise("x%d" % z, picked[:].rearrange("p s u -> p (s u)").bitcast(BF16), S))
-
+        whole = slice(0, P)
         hidden = [psum.tile([P, PACK, CHUNK], F32, name="hidden%d" % c) for c in range(CHUNKS)]
-        for z in range(PASSES):
-            grouped = sbuf("w2_grouped%d" % z, [P, PACK, P * PACK], BF16)
-            dst = grouped[:].rearrange("p t (m j) -> p m j t", j=PACK)
-            src = w2_raw[z][:].rearrange("p j (m t) -> p m j t", t=PACK)
-            split = W2_VECTOR_COLS[z]
-            nc.scalar.copy(out=dst[:, split:], in_=src[:, split:])
-            nc.vector.tensor_copy(out=dst[:, :split], in_=src[:, :split])
-            w2q = [quantise("w2_%d%d" % (z, t), grouped[:, t, :], P) for t in range(PACK)]
-            for c in range(CHUNKS):
-                for t in range(PACK):
-                    mx_pass(hidden[c][:, t, :], w2q[t], slice(0, P), xq[z], slice(c * CHUNK, (c + 1) * CHUNK),
-                            start=(z == 0 and t == 0), stop=(z == PASSES - 1 and t == PACK - 1))
+        acc = [psum.tile([P, CHUNK], F32, name="acc%d" % c) for c in range(CHUNKS)]
 
+        def gather_pass(z):
+            picked = sbuf("picked%d" % z, [P, 2, S], U32)
+            for u in range(2):
+                window = token_pairs(z, u, "x_raw%d%d" % (z, u), "window%d%d" % (z, u))
+                nc.vector.tensor_copy(out=picked[:, u, :], in_=window.indirect(offsets[:]))
+            return picked
+
+        def weave(name, picked, tokens):
+            woven = sbuf(name, [P, (tokens.stop - tokens.start) * PACK], BF16)
+            nc.vector.tensor_copy(
+                out=woven[:].bitcast(I32).rearrange("p (s u) -> p s u", u=2),
+                in_=picked[:, :, tokens].bitcast(I32).rearrange("p u s -> p s u"),
+            )
+            return woven
+
+        picked = gather_pass(0)
+        grouped = cast_w2(0, "w2_raw0", "w2_grouped0")
+        xq0 = quantise("x0", weave("woven0", picked, slice(0, S))[:], S)
+        w2q = quantise_w2(0, grouped)
+        for c in range(CHUNKS):
+            for t in range(PACK):
+                mx_pass(hidden[c][:, t, :], w2q[t], whole, xq0, slice(c * CHUNK, (c + 1) * CHUNK), start=(t == 0), stop=False)
+
+        picked = gather_pass(1)
+        grouped = cast_w2(1, "w2_raw1", "w2_grouped1")
+        woven = [weave("woven1%d" % half, picked, slice(half * HALF, (half + 1) * HALF)) for half in range(2)]
+        xq1 = [quantise("x10", woven[0][:], HALF)]
+        w2q = quantise_w2(1, grouped)
+        xq1.append(quantise("x11", woven[1][:], HALF))
+        for c in range(CHUNKS):
+            for t in range(PACK):
+                mx_pass(hidden[c][:, t, :], w2q[t], whole, xq1[c // 2], slice(c % 2 * CHUNK, (c % 2 + 1) * CHUNK), start=False, stop=(t == PACK - 1))
+
+        w1_raw = load("w1_raw", [P, PASSES, PACK, N], w1.rearrange("(z p j) n -> p z j n", z=PASSES, j=PACK))
         w1_grouped = sbuf("w1_grouped", [P, PASSES * N * PACK], BF16)
-        nc.vector.tensor_copy(
+        nc.scalar.copy(
             out=w1_grouped[:].rearrange("p (z c i j) -> p z c j i", z=PASSES, i=4, j=PACK),
             in_=w1_raw[:].rearrange("p z j (c i) -> p z c j i", i=4),
         )
-        w3_grouped = sbuf("w3_grouped", [P, N * PACK], BF16)
+        w3_raw = load("w3_raw", [P, PACK, N], w3.rearrange("(p j) n -> p j n", j=PACK))
+        w3_grouped = sbuf("w2_grouped1", [P, N * PACK], BF16)
         nc.vector.tensor_copy(
             out=w3_grouped[:].rearrange("p (c i j) -> p c j i", i=4, j=PACK),
             in_=w3_raw[:].rearrange("p j (c i) -> p c j i", i=4),
@@ -112,16 +143,15 @@ def tile_picked_lora_gelu_e_kernel(tc, xT, w1, w2, w3, offs, out):
         w1q = quantise("w1", w1_grouped[:], PASSES * N)
         w3q = quantise("w3", w3_grouped[:], N)
 
-        acc = [psum.tile([P, CHUNK], F32, name="acc%d" % c) for c in range(CHUNKS)]
         for c in range(CHUNKS):
-            for z in range(PASSES):
-                mx_pass(acc[c][:], w1q, slice(z * N, (z + 1) * N), xq[z], slice(c * CHUNK, (c + 1) * CHUNK), start=(z == 0), stop=False)
+            mx_pass(acc[c][:], w1q, slice(0, N), xq0, slice(c * CHUNK, (c + 1) * CHUNK), start=True, stop=False)
+            mx_pass(acc[c][:], w1q, slice(N, 2 * N), xq1[c // 2], slice(c % 2 * CHUNK, (c % 2 + 1) * CHUNK), start=False, stop=False)
 
         for c in range(CHUNKS):
             act = sbuf("act%d" % c, [P, CHUNK * PACK], BF16)
             nc.scalar.activation(act[:].rearrange("p (n t) -> p n t", t=PACK), hidden[c][:].rearrange("p t n -> p n t"), GELU)
             hq = quantise("h%d" % c, act[:], CHUNK)
-            mx_pass(acc[c][:], w3q, slice(0, N), hq, slice(0, CHUNK), start=False, stop=True)
+            mx_pass(acc[c][:], w3q, whole, hq, whole, start=False, stop=True)
             result = sbuf("result%d" % c, [P, CHUNK], F32)
             nc.vector.tensor_copy(out=result[:], in_=acc[c][:])
             nc.sync.dma_start(out=out[:, c * CHUNK : (c + 1) * CHUNK], in_=result[:])

@@ -20,8 +20,8 @@ K_PASS = P * PACK
 PASSES = K // K_PASS
 CHUNK = 128
 CHUNKS = S // CHUNK
-X_VECTOR_TOKENS = (640, 640, 544, 448)
-W2_VECTOR_COLS = (32, 32)
+X_VECTOR_TOKENS = (640, 640, 320, 352)
+W2_VECTOR_COLS = (0, 48)
 HALF = S // 2
 
 
@@ -40,8 +40,8 @@ def tile_picked_lora_gelu_e_kernel(tc, xT, w1, w2, w3, offs, out):
             nc.sync.dma_start(out=raw[:], in_=rows)
             return raw
 
-        def quantise(name, grouped, words):
-            codes = sbuf(name + "_codes", [P, words], U32)
+        def quantise(name, grouped, words, slot=None):
+            codes = sbuf(slot or name + "_codes", [P, words], U32)
             scales = sbuf(name + "_scales", [P, words], U8)
             nc.vector.quantize_mx(out=codes[:].bitcast(FP8X4), scales=scales[:], in_=grouped)
             return codes, scales
@@ -70,21 +70,18 @@ def tile_picked_lora_gelu_e_kernel(tc, xT, w1, w2, w3, offs, out):
             shared_cast(window[:].rearrange("p (t e) -> p t e", e=2), raw[:].rearrange("p e t -> p t e"), X_VECTOR_TOKENS[2 * z + u])
             return window[:].bitcast(U32)
 
-        def cast_w2(z, raw_slot, grouped_slot):
+        def cast_w2(z, raw_slot, grouped):
             raw = load(raw_slot, [P, PACK, H], w2[z * K_PASS : (z + 1) * K_PASS, :].rearrange("(p j) c -> p j c", j=PACK))
-            grouped = sbuf(grouped_slot, [P, H * PACK], BF16)
             shared_cast(
-                grouped[:].rearrange("p (t m j) -> p m j t", t=PACK, j=PACK),
+                grouped.rearrange("p (t m j) -> p m j t", t=PACK, j=PACK),
                 raw[:].rearrange("p j (m t) -> p m j t", t=PACK),
                 W2_VECTOR_COLS[z],
             )
-            return grouped
 
         def quantise_w2(z, grouped):
             return [quantise("w2_%d%d" % (z, t), grouped[:, t * K_PASS : (t + 1) * K_PASS], P) for t in range(PACK)]
 
         offsets = sb.tile([P, S // 16], U16, name="offsets")
-        nc.sync.dma_start(offsets[:], offs)
 
         warm_in = sbuf("warm_in", [P, 16], F32)
         warm_out = sbuf("warm_out", [P, 16], F32)
@@ -95,57 +92,64 @@ def tile_picked_lora_gelu_e_kernel(tc, xT, w1, w2, w3, offs, out):
         hidden = [psum.tile([P, PACK, CHUNK], F32, name="hidden%d" % c) for c in range(CHUNKS)]
         acc = [psum.tile([P, CHUNK], F32, name="acc%d" % c) for c in range(CHUNKS)]
 
-        def gather_pass(z):
-            picked = sbuf("picked%d" % z, [P, 2, S], U32)
-            for u in range(2):
-                window = token_pairs(z, u, "x_raw%d%d" % (z, u), "window%d%d" % (z, u))
-                nc.vector.tensor_copy(out=picked[:, u, :], in_=window.indirect(offsets[:]))
-            return picked
-
-        def weave(name, picked, tokens):
-            woven = sbuf(name, [P, (tokens.stop - tokens.start) * PACK], BF16)
+        def weave(woven, picked, tokens):
             nc.vector.tensor_copy(
-                out=woven[:].bitcast(I32).rearrange("p (s u) -> p s u", u=2),
+                out=woven.bitcast(I32).rearrange("p (s u) -> p s u", u=2),
                 in_=picked[:, :, tokens].bitcast(I32).rearrange("p u s -> p s u"),
             )
-            return woven
 
-        picked = gather_pass(0)
-        grouped = cast_w2(0, "w2_raw0", "w2_grouped0")
-        xq0 = quantise("x0", weave("woven0", picked, slice(0, S))[:], S)
-        w2q = quantise_w2(0, grouped)
-        for c in range(CHUNKS):
-            for t in range(PACK):
-                mx_pass(hidden[c][:, t, :], w2q[t], whole, xq0, slice(c * CHUNK, (c + 1) * CHUNK), start=(t == 0), stop=False)
+        picked = [sbuf("picked%d" % z, [P, 2, S], U32) for z in range(PASSES)]
 
-        picked = gather_pass(1)
-        grouped = cast_w2(1, "w2_raw1", "w2_grouped1")
-        woven = [weave("woven1%d" % half, picked, slice(half * HALF, (half + 1) * HALF)) for half in range(2)]
-        xq1 = [quantise("x10", woven[0][:], HALF)]
-        w2q = quantise_w2(1, grouped)
-        xq1.append(quantise("x11", woven[1][:], HALF))
-        for c in range(CHUNKS):
-            for t in range(PACK):
-                mx_pass(hidden[c][:, t, :], w2q[t], whole, xq1[c // 2], slice(c % 2 * CHUNK, (c % 2 + 1) * CHUNK), start=False, stop=(t == PACK - 1))
+        def gather(z, u, window):
+            nc.vector.tensor_copy(out=picked[z][:, u, :], in_=window.indirect(offsets[:]))
 
+        window = token_pairs(0, 0, "x_raw00", "window00")
+        nc.sync.dma_start(offsets[:], offs)
+        gather(0, 0, window)
+        gather(0, 1, token_pairs(0, 1, "x_raw01", "window01"))
+        woven = [sbuf("woven%d" % z, [P, S * PACK], BF16) for z in range(PASSES)]
+        weave(woven[0][:], picked[0], slice(0, S))
+        x0_early = quantise("x0_early", woven[0][:, : HALF * PACK], HALF)
+        for u in range(2):
+            gather(1, u, token_pairs(1, u, "x_raw1%d" % u, "window1%d" % u))
+        weave(woven[1][:], picked[1], slice(0, S))
+        x1 = quantise("x1", woven[1][:], S)
+
+        grouped = [sbuf("w2_grouped%d" % z, [P, H * PACK], BF16)[:] for z in range(PASSES)]
+        cast_w2(0, "w2_raw0", grouped[0])
+        w2q0 = [quantise("w2_0%d" % v, grouped[0][:, 2 * v * K_PASS : 2 * (v + 1) * K_PASS], 2 * P) for v in range(2)]
+        cast_w2(1, "w2_raw1", grouped[1])
+        w2q = [[(w2q0[t // 2], slice(t % 2 * P, (t % 2 + 1) * P)) for t in range(PACK)], [(q, whole) for q in quantise_w2(1, grouped[1])]]
+        x0_late = quantise("x0_late", woven[0][:, HALF * PACK :], HALF, slot="w2_raw1")
         w1_raw = load("w1_raw", [P, PASSES, PACK, N], w1.rearrange("(z p j) n -> p z j n", z=PASSES, j=PACK))
+        w3_raw = load("w3_raw", [P, PACK, N], w3.rearrange("(p j) n -> p j n", j=PACK))
+        w3_grouped = sbuf("w3_grouped", [P, N * PACK], BF16)[:]
+        nc.vector.tensor_copy(
+            out=w3_grouped.rearrange("p (c i j) -> p c j i", i=4, j=PACK),
+            in_=w3_raw[:].rearrange("p j (c i) -> p c j i", i=4),
+        )
+
+        def tokens(z, c):
+            if z == 0:
+                return (x0_early, x0_late)[c // 2], slice(c % 2 * CHUNK, (c % 2 + 1) * CHUNK)
+            return x1, slice(c * CHUNK, (c + 1) * CHUNK)
+
+        for c in range(CHUNKS):
+            for z in range(PASSES):
+                for t in range(PACK):
+                    mx_pass(hidden[c][:, t, :], *w2q[z][t], *tokens(z, c), start=(z == 0 and t == 0), stop=(z == 1 and t == PACK - 1))
+
         w1_grouped = sbuf("w1_grouped", [P, PASSES * N * PACK], BF16)
         nc.scalar.copy(
             out=w1_grouped[:].rearrange("p (z c i j) -> p z c j i", z=PASSES, i=4, j=PACK),
             in_=w1_raw[:].rearrange("p z j (c i) -> p z c j i", i=4),
         )
-        w3_raw = load("w3_raw", [P, PACK, N], w3.rearrange("(p j) n -> p j n", j=PACK))
-        w3_grouped = sbuf("w2_grouped1", [P, N * PACK], BF16)
-        nc.vector.tensor_copy(
-            out=w3_grouped[:].rearrange("p (c i j) -> p c j i", i=4, j=PACK),
-            in_=w3_raw[:].rearrange("p j (c i) -> p c j i", i=4),
-        )
         w1q = quantise("w1", w1_grouped[:], PASSES * N)
-        w3q = quantise("w3", w3_grouped[:], N)
+        w3q = quantise("w3", w3_grouped, N)
 
         for c in range(CHUNKS):
-            mx_pass(acc[c][:], w1q, slice(0, N), xq0, slice(c * CHUNK, (c + 1) * CHUNK), start=True, stop=False)
-            mx_pass(acc[c][:], w1q, slice(N, 2 * N), xq1[c // 2], slice(c % 2 * CHUNK, (c % 2 + 1) * CHUNK), start=False, stop=False)
+            mx_pass(acc[c][:], w1q, slice(0, N), *tokens(0, c), start=True, stop=False)
+            mx_pass(acc[c][:], w1q, slice(N, 2 * N), *tokens(1, c), start=False, stop=False)
 
         for c in range(CHUNKS):
             act = sbuf("act%d" % c, [P, CHUNK * PACK], BF16)

@@ -21,7 +21,7 @@ PASSES = K // K_PASS
 CHUNK = 128
 CHUNKS = S // CHUNK
 X_VECTOR_TOKENS = (640, 640, 320, 352)
-W2_VECTOR_COLS = (0, 48)
+W2_VECTOR_COLS = (60, 48)
 HALF = S // 2
 
 
@@ -107,20 +107,22 @@ def tile_picked_lora_gelu_e_kernel(tc, xT, w1, w2, w3, offs, out):
         nc.sync.dma_start(offsets[:], offs)
         gather(0, 0, window)
         gather(0, 1, token_pairs(0, 1, "x_raw01", "window01"))
-        woven = [sbuf("woven%d" % z, [P, S * PACK], BF16) for z in range(PASSES)]
-        weave(woven[0][:], picked[0], slice(0, S))
-        x0_early = quantise("x0_early", woven[0][:, : HALF * PACK], HALF)
+        woven = sbuf("woven0", [P, S * PACK], BF16)
+        weave(woven[:], picked[0], slice(0, S))
+        x0 = quantise("x0", woven[:], S)
         for u in range(2):
             gather(1, u, token_pairs(1, u, "x_raw1%d" % u, "window1%d" % u))
-        weave(woven[1][:], picked[1], slice(0, S))
-        x1 = quantise("x1", woven[1][:], S)
 
         grouped = [sbuf("w2_grouped%d" % z, [P, H * PACK], BF16)[:] for z in range(PASSES)]
         cast_w2(0, "w2_raw0", grouped[0])
         w2q0 = [quantise("w2_0%d" % v, grouped[0][:, 2 * v * K_PASS : 2 * (v + 1) * K_PASS], 2 * P) for v in range(2)]
+        woven = sbuf("w2_raw0", [P, S * PACK], BF16)
+        for half in range(2):
+            weave(woven[:, half * HALF * PACK : (half + 1) * HALF * PACK], picked[1], slice(half * HALF, (half + 1) * HALF))
+        x1_early = quantise("x1_early", woven[:, : HALF * PACK], HALF)
         cast_w2(1, "w2_raw1", grouped[1])
         w2q = [[(w2q0[t // 2], slice(t % 2 * P, (t % 2 + 1) * P)) for t in range(PACK)], [(q, whole) for q in quantise_w2(1, grouped[1])]]
-        x0_late = quantise("x0_late", woven[0][:, HALF * PACK :], HALF, slot="w2_raw1")
+        x1_late = quantise("x1_late", woven[:, HALF * PACK :], HALF, slot="w2_raw1")
         w1_raw = load("w1_raw", [P, PASSES, PACK, N], w1.rearrange("(z p j) n -> p z j n", z=PASSES, j=PACK))
         w3_raw = load("w3_raw", [P, PACK, N], w3.rearrange("(p j) n -> p j n", j=PACK))
         w3_grouped = sbuf("w3_grouped", [P, N * PACK], BF16)[:]
@@ -131,8 +133,8 @@ def tile_picked_lora_gelu_e_kernel(tc, xT, w1, w2, w3, offs, out):
 
         def tokens(z, c):
             if z == 0:
-                return (x0_early, x0_late)[c // 2], slice(c % 2 * CHUNK, (c % 2 + 1) * CHUNK)
-            return x1, slice(c * CHUNK, (c + 1) * CHUNK)
+                return x0, slice(c * CHUNK, (c + 1) * CHUNK)
+            return (x1_early, x1_late)[c // 2], slice(c % 2 * CHUNK, (c % 2 + 1) * CHUNK)
 
         for c in range(CHUNKS):
             for z in range(PASSES):

from contextlib import ExitStack

import concourse.mybir as mybir

K, T, S, H, N = 1024, 1024, 512, 512, 128
FLOPS = 2 * S * (K * H + K * N + H * N)

F32 = mybir.dt.float32
BF16 = mybir.dt.bfloat16
U32 = mybir.dt.uint32
I32 = mybir.dt.int32
U16 = mybir.dt.uint16
U8 = mybir.dt.uint8
FP8X4 = mybir.dt.float8_e4m3fn_x4
GELU = mybir.ActivationFunctionType.Gelu_apprx_tanh

P = 128
PACK = 4
K_PASS = P * PACK
PASSES = K // K_PASS
CHUNK = 128
CHUNKS = S // CHUNK
X_VECTOR_TOKENS = (640, 640, 320, 352)
W2_VECTOR_COLS = (60, 48)
HALF = S // 2


def tile_picked_lora_gelu_e_kernel(tc, xT, w1, w2, w3, offs, out):
    nc = tc.nc

    with ExitStack() as ctx:
        sb = ctx.enter_context(tc.tile_pool(name="sb", bufs=1))
        psum = ctx.enter_context(tc.psum_pool(name="psum", bufs=1))

        def sbuf(name, shape, dtype):
            return sb.tile(shape, dtype, name=name, align_bytes=64)

        def load(slot, shape, rows):
            raw = sbuf(slot, shape, F32)
            nc.sync.dma_start(out=raw[:], in_=rows)
            return raw

        def quantise(name, grouped, words, slot=None):
            codes = sbuf(slot or name + "_codes", [P, words], U32)
            scales = sbuf(name + "_scales", [P, words], U8)
            nc.vector.quantize_mx(out=codes[:].bitcast(FP8X4), scales=scales[:], in_=grouped)
            return codes, scales

        def mx_pass(dst, stationary, s_cols, moving, m_cols, start, stop):
            nc.tensor.matmul_mx(
                out=dst,
                lhsT=stationary[0][:, s_cols].bitcast(FP8X4),
                lhsT_scale=stationary[1][:, s_cols],
                rhs=moving[0][:, m_cols].bitcast(FP8X4),
                rhs_scale=moving[1][:, m_cols],
                start=start,
                stop=stop,
            )

        def shared_cast(dst, src, split):
            nc.scalar.copy(out=dst[:, split:], in_=src[:, split:])
            if split:
                nc.vector.tensor_copy(out=dst[:, :split], in_=src[:, :split])

        x_rows = xT.rearrange("(z p u e) t -> z u p e t", z=PASSES, p=P, u=2)

        def token_pairs(z, u, raw_slot, window_slot):
            raw = load(raw_slot, [P, 2, T], x_rows[z, u])
            window = sbuf(window_slot, [P, 2 * T], BF16)
            shared_cast(window[:].rearrange("p (t e) -> p t e", e=2), raw[:].rearrange("p e t -> p t e"), X_VECTOR_TOKENS[2 * z + u])
            return window[:].bitcast(U32)

        def cast_w2(z, raw_slot, grouped):
            raw = load(raw_slot, [P, PACK, H], w2[z * K_PASS : (z + 1) * K_PASS, :].rearrange("(p j) c -> p j c", j=PACK))
            shared_cast(
                grouped.rearrange("p (t m j) -> p m j t", t=PACK, j=PACK),
                raw[:].rearrange("p j (m t) -> p m j t", t=PACK),
                W2_VECTOR_COLS[z],
            )

        def quantise_w2(z, grouped):
            return [quantise("w2_%d%d" % (z, t), grouped[:, t * K_PASS : (t + 1) * K_PASS], P) for t in range(PACK)]

        offsets = sb.tile([P, S // 16], U16, name="offsets")

        warm_in = sbuf("warm_in", [P, 16], F32)
        warm_out = sbuf("warm_out", [P, 16], F32)
        nc.vector.memset(warm_in[:], 0.0)
        nc.scalar.activation(warm_out[:], warm_in[:], GELU)

        whole = slice(0, P)
        hidden = [psum.tile([P, PACK, CHUNK], F32, name="hidden%d" % c) for c in range(CHUNKS)]
        acc = [psum.tile([P, CHUNK], F32, name="acc%d" % c) for c in range(CHUNKS)]

        def weave(woven, picked, tokens):
            nc.vector.tensor_copy(
                out=woven.bitcast(I32).rearrange("p (s u) -> p s u", u=2),
                in_=picked[:, :, tokens].bitcast(I32).rearrange("p u s -> p s u"),
            )

        picked = [sbuf("picked%d" % z, [P, 2, S], U32) for z in range(PASSES)]

        def gather(z, u, window):
            nc.vector.tensor_copy(out=picked[z][:, u, :], in_=window.indirect(offsets[:]))

        window = token_pairs(0, 0, "x_raw00", "window00")
        nc.sync.dma_start(offsets[:], offs)
        gather(0, 0, window)
        gather(0, 1, token_pairs(0, 1, "x_raw01", "window01"))
        woven = sbuf("woven0", [P, S * PACK], BF16)
        weave(woven[:], picked[0], slice(0, S))
        x0 = quantise("x0", woven[:], S)
        for u in range(2):
            gather(1, u, token_pairs(1, u, "x_raw1%d" % u, "window1%d" % u))

        grouped = [sbuf("w2_grouped%d" % z, [P, H * PACK], BF16)[:] for z in range(PASSES)]
        cast_w2(0, "w2_raw0", grouped[0])
        w2q0 = [quantise("w2_0%d" % v, grouped[0][:, 2 * v * K_PASS : 2 * (v + 1) * K_PASS], 2 * P) for v in range(2)]
        woven = sbuf("w2_raw0", [P, S * PACK], BF16)
        for half in range(2):
            weave(woven[:, half * HALF * PACK : (half + 1) * HALF * PACK], picked[1], slice(half * HALF, (half + 1) * HALF))
        x1_early = quantise("x1_early", woven[:, : HALF * PACK], HALF)
        cast_w2(1, "w2_raw1", grouped[1])
        w2q = [[(w2q0[t // 2], slice(t % 2 * P, (t % 2 + 1) * P)) for t in range(PACK)], [(q, whole) for q in quantise_w2(1, grouped[1])]]
        x1_late = quantise("x1_late", woven[:, HALF * PACK :], HALF, slot="w2_raw1")
        w1_raw = load("w1_raw", [P, PASSES, PACK, N], w1.rearrange("(z p j) n -> p z j n", z=PASSES, j=PACK))
        w3_raw = load("w3_raw", [P, PACK, N], w3.rearrange("(p j) n -> p j n", j=PACK))
        w3_grouped = sbuf("w3_grouped", [P, N * PACK], BF16)[:]
        nc.vector.tensor_copy(
            out=w3_grouped.rearrange("p (c i j) -> p c j i", i=4, j=PACK),
            in_=w3_raw[:].rearrange("p j (c i) -> p c j i", i=4),
        )

        def tokens(z, c):
            if z == 0:
                return x0, slice(c * CHUNK, (c + 1) * CHUNK)
            return (x1_early, x1_late)[c // 2], slice(c % 2 * CHUNK, (c % 2 + 1) * CHUNK)

        for c in range(CHUNKS):
            for z in range(PASSES):
                for t in range(PACK):
                    mx_pass(hidden[c][:, t, :], *w2q[z][t], *tokens(z, c), start=(z == 0 and t == 0), stop=(z == 1 and t == PACK - 1))

        w1_grouped = sbuf("w1_grouped", [P, PASSES * N * PACK], BF16)
        nc.scalar.copy(
            out=w1_grouped[:].rearrange("p (z c i j) -> p z c j i", z=PASSES, i=4, j=PACK),
            in_=w1_raw[:].rearrange("p z j (c i) -> p z c j i", i=4),
        )
        w1q = quantise("w1", w1_grouped[:], PASSES * N)
        w3q = quantise("w3", w3_grouped, N)

        for c in range(CHUNKS):
            mx_pass(acc[c][:], w1q, slice(0, N), *tokens(0, c), start=True, stop=False)
            mx_pass(acc[c][:], w1q, slice(N, 2 * N), *tokens(1, c), start=False, stop=False)

        for c in range(CHUNKS):
            act = sbuf("act%d" % c, [P, CHUNK * PACK], BF16)
            nc.scalar.activation(act[:].rearrange("p (n t) -> p n t", t=PACK), hidden[c][:].rearrange("p t n -> p n t"), GELU)
            hq = quantise("h%d" % c, act[:], CHUNK)
            mx_pass(acc[c][:], w3q, whole, hq, whole, start=False, stop=True)
            result = sbuf("result%d" % c, [P, CHUNK], F32)
            nc.vector.tensor_copy(out=result[:], in_=acc[c][:])
            nc.sync.dma_start(out=out[:, c * CHUNK : (c + 1) * CHUNK], in_=result[:])
